import numpy as np
import ml_dtypes


def mxq(x, axis, fmt="e4m3"):
    dtype, down = {"e4m3": (ml_dtypes.float8_e4m3fn, 7), "e5m2": (ml_dtypes.float8_e5m2, 14)}[fmt]
    v = np.moveaxis(np.asarray(x, np.float32).astype(ml_dtypes.bfloat16).astype(np.float64), axis, -1)
    blocks = v.reshape(v.shape[:-1] + (-1, 32))
    amax = np.abs(blocks).max(-1, keepdims=True)
    byte = np.maximum(np.where(amax > 0, np.frexp(amax)[1] - 1 + 127, 0) - down, 1)
    scale = np.exp2(byte - 127.0)
    codes = (blocks / scale).astype(np.float32).astype(dtype).astype(np.float64)
    return np.moveaxis((codes * scale).reshape(v.shape), -1, axis)


WIDE = False


def mx_kscale(k, group=512):
    if not WIDE:
        return np.ones(k)
    levels = np.array([10, -10, 5, -5, 0])
    if group != 512:
        return np.exp2(np.random.permutation(np.resize(levels, k // group))).repeat(group)
    if k % 512:
        return np.exp2(np.random.permutation(np.resize(levels, k // 32))).repeat(32)
    a = np.empty((k // 512, 16))
    for p in range(k // 512):
        a[p, :8] = np.random.permutation(np.resize(levels, 8))
        for g in range(8):
            far = levels[np.abs(levels - a[p, g]) >= 10]
            a[p, g + 8] = far[np.random.randint(len(far))]
    return np.exp2(a.ravel()).repeat(32)


def f64(x):
    return np.asarray(x).astype(np.float64)


E2M1 = np.array([0.0, 0.5, 1.0, 1.5, 2.0, 3.0, 4.0, 6.0, -0.0, -0.5, -1.0, -1.5, -2.0, -3.0, -4.0, -6.0])


def pack_group(w):
    k, n = w.shape
    w = f64(np.asarray(w, np.float32).astype(ml_dtypes.bfloat16)).reshape(k // 32, 32, n)
    amax = np.abs(w).max(1)
    mant, ex = np.frexp(amax / 6.0)
    byte = np.clip(np.where(amax > 0, np.where(mant > 0.5, ex, ex - 1) + 127, 1), 1, 254)
    scaled = (w * np.exp2(127.0 - byte)[:, None, :]).reshape(k, n).astype(np.float32)
    c = np.ascontiguousarray(scaled.reshape(k // 4, 4, n).transpose(0, 2, 1)).astype(ml_dtypes.float4_e2m1fn).view(np.uint8) & 0xF
    return np.ascontiguousarray((c[..., 0::2] | (c[..., 1::2] << 4)).reshape(k // 4, 2 * n)), byte.astype(np.uint8)


def unpack_group(words, scales):
    p, n = words.shape[0], scales.shape[1]
    words = np.ascontiguousarray(words).reshape(p, n, 2)
    nib = np.empty((p, n, 4), np.uint8)
    nib[..., 0::2] = words & 0xF
    nib[..., 1::2] = words >> 4
    return E2M1[nib].transpose(0, 2, 1).reshape(4 * p, n) * np.repeat(np.exp2(scales.astype(np.float64) - 127.0), 32, axis=0)


G, D, M, O, N = 2, 256, 256, 256, 512


def setup_inputs():
    n = np.random.standard_normal
    s_d = mx_kscale(D, 0)
    s_o = mx_kscale(O, 0)
    w1_ = [pack_group(w) for w in n((G, D, M)) / np.sqrt(D) / s_d[:, None]]
    w2_ = [pack_group(w) for w in n((G, D, M)) / np.sqrt(D) / s_d[:, None]]
    w3_ = [pack_group(w) for w in n((G, D, M)) / np.sqrt(D) / s_d[:, None]]
    wo_ = [pack_group(w) for w in n((G, O, M)) / np.sqrt(O) / s_o[:, None]]
    return {
        "x": (n((G, D, N)) * s_d[:, None]).astype(np.float32),
        "w1_words": np.stack([w[0] for w in w1_]),
        "w1_scales": np.stack([w[1] for w in w1_]),
        "w2_words": np.stack([w[0] for w in w2_]),
        "w2_scales": np.stack([w[1] for w in w2_]),
        "w3_words": np.stack([w[0] for w in w3_]),
        "w3_scales": np.stack([w[1] for w in w3_]),
        "re": (np.random.uniform(0.3, 1.5, (G, M, 1))).astype(np.float32),
        "wo_words": np.stack([w[0] for w in wo_]),
        "wo_scales": np.stack([w[1] for w in wo_]),
        "dy": (n((G, O, N)) * s_o[:, None]).astype(np.float32),
        "old": (0.3 * n((G, M, N))).astype(np.float32),
    }


def reference(x, w1_words, w1_scales, w2_words, w2_scales, w3_words, w3_scales, re, wo_words, wo_scales, dy, old):
    w1 = np.stack([unpack_group(w1_words[g], w1_scales[g]) for g in range(G)])
    xq = mxq(f64(x), 1, "e4m3")
    z1 = w1.transpose(0, 2, 1) @ xq
    w2 = np.stack([unpack_group(w2_words[g], w2_scales[g]) for g in range(G)])
    z2 = w2.transpose(0, 2, 1) @ xq
    w3 = np.stack([unpack_group(w3_words[g], w3_scales[g]) for g in range(G)])
    z3 = w3.transpose(0, 2, 1) @ xq
    e1 = np.exp(z1)
    e2 = np.exp(z2)
    wo = np.stack([unpack_group(wo_words[g], wo_scales[g]) for g in range(G)])
    dyq = mxq(f64(dy), 1, "e4m3")
    c0 = wo.transpose(0, 2, 1) @ dyq
    de1 = c0 * z3 / (e1 + e2 + f64(re)) - c0 * z3 * e1 / np.square(e1 + e2 + f64(re))
    dz1 = de1 * e1
    y = dz1 + f64(old)
    return y

@@ -1,0 +1,160 @@
+from contextlib import ExitStack
+
+import concourse.mybir as mybir
+
+G, D, M, N = 2, 256, 256, 512
+FLOPS = 4 * 2 * G * D * M * N
+
+F32 = mybir.dt.float32
+BF16 = mybir.dt.bfloat16
+I32 = mybir.dt.int32
+U32 = mybir.dt.uint32
+U8 = mybir.dt.uint8
+FP8X4 = mybir.dt.float8_e4m3fn_x4
+FP4X4 = mybir.dt.float4_e2m1fn_x4
+ACT = mybir.ActivationFunctionType
+ALU = mybir.AluOpType
+
+P = 128
+PACK = 4
+ROWS = D // PACK
+HALVES = M // P
+TILES = [(g, h) for h in range(HALVES) for g in range(G)]
+X_SPLIT = 336
+R_CAP = 1e30
+
+
+def tile_rows_btwoshare_kernel(tc, x, w1_words, w1_scales, w2_words, w2_scales, w3_words, w3_scales,
+                                   re, wo_words, wo_scales, dy, old, out):
+    nc = tc.nc
+    with ExitStack() as ctx:
+        sb = ctx.enter_context(tc.tile_pool(name="sb", bufs=1))
+        ps = ctx.enter_context(tc.psum_pool(name="ps", bufs=1))
+        ctx.enter_context(tc.manual_schedule())
+
+        names = ["w1", "w2", "w3", "wo"]
+        words = {k: sb.tile([P, 2 * M], U8, name="words_" + k, align_bytes=64) for k in names}
+        acts = ["x", "dy"]
+        plane = {k: sb.tile([P, N if k in acts else M], U8, name="plane_" + k, align_bytes=64) for k in names + acts}
+        raw = {k: sb.tile([P, PACK, N], F32, name="raw_" + k, align_bytes=64) for k in acts}
+        grouped = {k: sb.tile([P, N, PACK], BF16, name="grouped_" + k, align_bytes=64) for k in acts}
+        codes = {k: sb.tile([P, N], U32, name="codes_" + k, align_bytes=64) for k in acts}
+        re_sb = sb.tile([P, G * HALVES], F32, name="re_sb")
+        old_sb = sb.tile([P, G * HALVES, N], F32, name="old_sb")
+        bank_a = [ps.tile([P, N], F32, name="bank_a%d" % t) for t in range(4)]
+        bank_b = [ps.tile([P, N], F32, name="bank_b%d" % t) for t in range(4)]
+
+        def work(label):
+            return [sb.tile([P, N], F32, name="%s%d" % (label, t), align_bytes=64) for t in range(4)]
+
+        inv_e1, e2, ratio, grad, root, inv_s, res = [work(s) for s in
+            ["inv_e1", "e2", "ratio", "grad", "root", "inv_s", "res"]]
+        inv_s2 = root
+
+        def load_words(eng, k, src):
+            eng.dma_start(out=words[k][:].bitcast(I32), in_=src.rearrange("g p b -> (g p) b").bitcast(I32))
+
+        def load_plane(eng, k, src):
+            rows = src.rearrange("g (u r) m -> r (g u) m", r=4)
+            for r in range(4):
+                eng.dma_start(out=plane[k][r:P:32, :].bitcast(I32), in_=rows[r].bitcast(I32))
+
+        def load_act(k, src):
+            nc.sync.dma_start(out=raw[k][:], in_=src.rearrange("g (p j) n -> (g p) j n", j=PACK))
+
+        def views(k, lo, hi):
+            return (grouped[k][:, lo:hi, :].rearrange("p (c i) j -> p c j i", i=4),
+                    raw[k][:, :, lo:hi].rearrange("p j (c i) -> p c j i", i=4))
+
+        def quantize(k):
+            nc.vector.quantize_mx(out=codes[k][:].bitcast(FP8X4), scales=plane[k][:],
+                                  in_=grouped[k][:].rearrange("p n j -> p (n j)"))
+
+        def product(bank, t, w, a):
+            g, h = TILES[t]
+            rows = slice(ROWS * g, ROWS * (g + 1))
+            nc.tensor.matmul_mx(out=bank[t][:],
+                                lhsT=words[w][rows, 2 * P * h:2 * P * (h + 1)].bitcast(FP4X4),
+                                lhsT_scale=plane[w][rows, P * h:P * (h + 1)],
+                                rhs=codes[a][rows, :].bitcast(FP8X4), rhs_scale=plane[a][rows, :],
+                                start=True, stop=True)
+
+        def col(t):
+            g, h = TILES[t]
+            return HALVES * g + h
+
+        nc.vector.memset(plane["w1"][:].bitcast(I32), 0)
+        nc.gpsimd.memset(plane["w2"][:].bitcast(I32), 0)
+        nc.vector.memset(plane["w3"][:].bitcast(I32), 0)
+        nc.vector.memset(plane["wo"][:].bitcast(I32), 0)
+        load_act("x", x)
+        load_act("dy", dy)
+        load_words(nc.scalar, "w1", w1_words)
+        load_words(nc.scalar, "w2", w2_words)
+        load_plane(nc.scalar, "w1", w1_scales)
+        load_plane(nc.gpsimd, "w2", w2_scales)
+        load_words(nc.sync, "w3", w3_words)
+        load_plane(nc.sync, "w3", w3_scales)
+        with nc.allow_non_contiguous_dma(reason="one reserve a partition"):
+            nc.sync.dma_start(out=re_sb[:], in_=re.rearrange("g (h p) o -> p (g h o)", p=P))
+        load_words(nc.sync, "wo", wo_words)
+        load_plane(nc.sync, "wo", wo_scales)
+        nc.sync.dma_start(out=old_sb[:], in_=old.rearrange("g (h p) n -> p (g h) n", p=P))
+
+        dst, src = views("x", 0, X_SPLIT)
+        nc.vector.tensor_copy(out=dst, in_=src)
+        dst, src = views("x", X_SPLIT, N)
+        nc.scalar.copy(out=dst, in_=src)
+        quantize("x")
+        dst, src = views("dy", 0, N)
+        nc.vector.tensor_copy(out=dst, in_=src)
+
+        def make_ratio(t):
+            nc.vector.scalar_tensor_tensor(out=ratio[t][:], in0=e2[t][:], scalar=re_sb[:, col(t):col(t) + 1],
+                                           in1=inv_e1[t][:], op0=ALU.add, op1=ALU.mult)
+
+        for pair in [(0, 1), (2, 3)]:
+            for t in pair:
+                product(bank_a, t, "w1", "x")
+            for t in pair:
+                product(bank_b, t, "w2", "x")
+            for t in pair:
+                nc.scalar.activation(out=inv_e1[t][:], in_=bank_a[t][:], func=ACT.Exp, scale=-1.0)
+            for t in pair:
+                nc.scalar.activation(out=e2[t][:], in_=bank_b[t][:], func=ACT.Exp)
+
+        make_ratio(0)
+        quantize("dy")
+        for pair in [(0, 1), (2, 3)]:
+            for t in pair:
+                if t > 0:
+                    make_ratio(t)
+            for t in pair:
+                product(bank_a, t, "w3", "x")
+            for t in pair:
+                product(bank_b, t, "wo", "dy")
+            for t in pair:
+                nc.vector.scalar_tensor_tensor(out=grad[t][:], in0=ratio[t][:], scalar=R_CAP,
+                                               in1=bank_a[t][:], op0=ALU.min, op1=ALU.mult)
+            for t in pair:
+                nc.vector.tensor_tensor(out=grad[t][:], in0=grad[t][:], in1=bank_b[t][:], op=ALU.mult)
+
+        halves = [slice(0, N // 2), slice(N // 2, N)]
+        for t in [0, 1, 3, 2]:
+            g, h = TILES[t]
+            for c in halves:
+                nc.scalar.activation(out=root[t][:, c], in_=ratio[t][:, c], func=ACT.Abs_reciprocal_sqrt, bias=1.0)
+            for c in halves:
+                nc.scalar.activation(out=inv_s[t][:, c], in_=root[t][:, c], func=ACT.Square)
+            if t == 3:
+                for rep in range(2):
+                    for c in halves:
+                        nc.vector.tensor_tensor(out=grad[t][:, c], in0=grad[t][:, c], in1=inv_s[t][:, c], op=ALU.mult)
+            else:
+                for c in halves:
+                    nc.scalar.activation(out=inv_s2[t][:, c], in_=inv_s[t][:, c], func=ACT.Square)
+                for c in halves:
+                    nc.vector.tensor_tensor(out=grad[t][:, c], in0=grad[t][:, c], in1=inv_s2[t][:, c], op=ALU.mult)
+            for c in halves:
+                nc.vector.tensor_tensor(out=res[t][:, c], in0=grad[t][:, c], in1=old_sb[:, col(t), c], op=ALU.add)
+            nc.sync.dma_start(out=out[g, P * h:P * (h + 1), :], in_=res[t][:])

@@ -20,6 +20,7 @@ PACK = 4
 ROWS = D // PACK
 HALVES = M // P
 TILES = [(g, h) for h in range(HALVES) for g in range(G)]
+CHUNKS = {"x": [slice(0, N)], "dy": [slice(0, N // 2), slice(N // 2, N)]}
 X_SPLIT = 336
 R_CAP = 1e30
 
@@ -36,10 +37,13 @@ def tile_rows_btwoshare_kernel(tc, x, w1_words, w1_scales, w2_words, w2_scales, 
         words = {k: sb.tile([P, 2 * M], U8, name="words_" + k, align_bytes=64) for k in names}
         acts = ["x", "dy"]
         plane = {k: sb.tile([P, N if k in acts else M], U8, name="plane_" + k, align_bytes=64) for k in names + acts}
-        raw = {k: sb.tile([P, PACK, N], F32, name="raw_" + k, align_bytes=64) for k in acts}
-        grouped = {k: sb.tile([P, N, PACK], BF16, name="grouped_" + k, align_bytes=64) for k in acts}
+        raw = {(k, c): sb.tile([P, PACK, cols.stop - cols.start], F32, name="raw_%s%d" % (k, c), align_bytes=64)
+               for k in acts for c, cols in enumerate(CHUNKS[k])}
+        grouped = {(k, c): sb.tile([P, cols.stop - cols.start, PACK], BF16, name="grouped_%s%d" % (k, c), align_bytes=64)
+                   for k in acts for c, cols in enumerate(CHUNKS[k])}
         codes = {k: sb.tile([P, N], U32, name="codes_" + k, align_bytes=64) for k in acts}
-        re_sb = sb.tile([P, G * HALVES], F32, name="re_sb")
+        re_rows = sb.tile([P, P], F32, name="re_rows", align_bytes=64)
+        re_sb = sb.tile([P, P], F32, name="re_sb", align_bytes=64)
         old_sb = sb.tile([P, G * HALVES, N], F32, name="old_sb")
         bank_a = [ps.tile([P, N], F32, name="bank_a%d" % t) for t in range(4)]
         bank_b = [ps.tile([P, N], F32, name="bank_b%d" % t) for t in range(4)]
@@ -59,16 +63,25 @@ def tile_rows_btwoshare_kernel(tc, x, w1_words, w1_scales, w2_words, w2_scales, 
             for r in range(4):
                 eng.dma_start(out=plane[k][r:P:32, :].bitcast(I32), in_=rows[r].bitcast(I32))
 
-        def load_act(k, src):
-            nc.sync.dma_start(out=raw[k][:], in_=src.rearrange("g (p j) n -> (g p) j n", j=PACK))
+        def load_act(k, c, src):
+            nc.sync.dma_start(out=raw[k, c][:], in_=src.rearrange("g (p j) n -> (g p) j n", j=PACK)[:, :, CHUNKS[k][c]])
 
-        def views(k, lo, hi):
-            return (grouped[k][:, lo:hi, :].rearrange("p (c i) j -> p c j i", i=4),
-                    raw[k][:, :, lo:hi].rearrange("p j (c i) -> p c j i", i=4))
+        def views(k, c, lo, hi):
+            return (grouped[k, c][:, lo:hi, :].rearrange("p (c i) j -> p c j i", i=4),
+                    raw[k, c][:, :, lo:hi].rearrange("p j (c i) -> p c j i", i=4))
 
-        def quantize(k):
-            nc.vector.quantize_mx(out=codes[k][:].bitcast(FP8X4), scales=plane[k][:],
-                                  in_=grouped[k][:].rearrange("p n j -> p (n j)"))
+        def group_v(k, c, lo, hi):
+            dst, src = views(k, c, lo, hi)
+            nc.vector.tensor_copy(out=dst, in_=src)
+
+        def group_s(k, c, lo, hi):
+            dst, src = views(k, c, lo, hi)
+            nc.scalar.copy(out=dst, in_=src)
+
+        def quantize(k, c):
+            cols = CHUNKS[k][c]
+            nc.vector.quantize_mx(out=codes[k][:, cols].bitcast(FP8X4), scales=plane[k][:, cols],
+                                  in_=grouped[k, c][:].rearrange("p n j -> p (n j)"))
 
         def product(bank, t, w, a):
             g, h = TILES[t]
@@ -83,34 +96,36 @@ def tile_rows_btwoshare_kernel(tc, x, w1_words, w1_scales, w2_words, w2_scales, 
             g, h = TILES[t]
             return HALVES * g + h
 
-        nc.vector.memset(plane["w1"][:].bitcast(I32), 0)
-        nc.gpsimd.memset(plane["w2"][:].bitcast(I32), 0)
-        nc.vector.memset(plane["w3"][:].bitcast(I32), 0)
+        for k in ["w1", "w2", "w3"]:
+            nc.gpsimd.memset(plane[k][:].bitcast(I32), 0)
         nc.vector.memset(plane["wo"][:].bitcast(I32), 0)
-        load_act("x", x)
-        load_act("dy", dy)
-        load_words(nc.scalar, "w1", w1_words)
-        load_words(nc.scalar, "w2", w2_words)
-        load_plane(nc.scalar, "w1", w1_scales)
-        load_plane(nc.gpsimd, "w2", w2_scales)
+        nc.vector.memset(re_rows[:], 0.0)
+        load_act("x", 0, x)
+        load_words(nc.sync, "w1", w1_words)
+        load_plane(nc.sync, "w1", w1_scales)
+        load_words(nc.sync, "w2", w2_words)
+        load_act("dy", 0, dy)
+        load_plane(nc.sync, "w2", w2_scales)
+        load_plane(nc.gpsimd, "w3", w3_scales)
+        load_act("dy", 1, dy)
+        nc.sync.dma_start(out=re_rows[0:P:32, :].rearrange("q (t i) -> q t i", i=32),
+                          in_=re.rearrange("g (h q i) o -> q (g h) (i o)", q=4, i=32))
         load_words(nc.sync, "w3", w3_words)
-        load_plane(nc.sync, "w3", w3_scales)
-        with nc.allow_non_contiguous_dma(reason="one reserve a partition"):
-            nc.sync.dma_start(out=re_sb[:], in_=re.rearrange("g (h p) o -> p (g h o)", p=P))
         load_words(nc.sync, "wo", wo_words)
         load_plane(nc.sync, "wo", wo_scales)
         nc.sync.dma_start(out=old_sb[:], in_=old.rearrange("g (h p) n -> p (g h) n", p=P))
 
-        dst, src = views("x", 0, X_SPLIT)
-        nc.vector.tensor_copy(out=dst, in_=src)
-        dst, src = views("x", X_SPLIT, N)
-        nc.scalar.copy(out=dst, in_=src)
-        quantize("x")
-        dst, src = views("dy", 0, N)
-        nc.vector.tensor_copy(out=dst, in_=src)
+        group_v("x", 0, 0, X_SPLIT)
+        group_s("x", 0, X_SPLIT, N)
+        quantize("x", 0)
+        group_v("dy", 0, 0, N // 2)
+        quantize("dy", 0)
+        group_v("dy", 1, 0, N // 2)
+        nc.vector.transpose(re_sb[:], re_rows[:])
+        quantize("dy", 1)
 
         def make_ratio(t):
-            nc.vector.scalar_tensor_tensor(out=ratio[t][:], in0=e2[t][:], scalar=re_sb[:, col(t):col(t) + 1],
+            nc.vector.scalar_tensor_tensor(out=ratio[t][:], in0=e2[t][:], scalar=re_sb[:, 32 * col(t):32 * col(t) + 1],
                                            in1=inv_e1[t][:], op0=ALU.add, op1=ALU.mult)
 
         for pair in [(0, 1), (2, 3)]:
@@ -123,38 +138,49 @@ def tile_rows_btwoshare_kernel(tc, x, w1_words, w1_scales, w2_words, w2_scales, 
             for t in pair:
                 nc.scalar.activation(out=e2[t][:], in_=bank_b[t][:], func=ACT.Exp)
 
-        make_ratio(0)
-        quantize("dy")
+        def times_z3(t):
+            nc.vector.scalar_tensor_tensor(out=grad[t][:], in0=ratio[t][:], scalar=R_CAP,
+                                           in1=bank_a[t][:], op0=ALU.min, op1=ALU.mult)
+
+        def times_c0(t):
+            nc.vector.tensor_tensor(out=grad[t][:], in0=grad[t][:], in1=bank_b[t][:], op=ALU.mult)
+
         for pair in [(0, 1), (2, 3)]:
-            for t in pair:
-                if t > 0:
-                    make_ratio(t)
             for t in pair:
                 product(bank_a, t, "w3", "x")
             for t in pair:
                 product(bank_b, t, "wo", "dy")
+        for step, pair in [(make_ratio, (0, 1)), (times_z3, (0, 1)), (make_ratio, (2, 3)), (times_c0, (0, 1)),
+                           (times_z3, (2, 3)), (times_c0, (2, 3))]:
             for t in pair:
-                nc.vector.scalar_tensor_tensor(out=grad[t][:], in0=ratio[t][:], scalar=R_CAP,
-                                               in1=bank_a[t][:], op0=ALU.min, op1=ALU.mult)
-            for t in pair:
-                nc.vector.tensor_tensor(out=grad[t][:], in0=grad[t][:], in1=bank_b[t][:], op=ALU.mult)
+                step(t)
 
-        halves = [slice(0, N // 2), slice(N // 2, N)]
-        for t in [0, 1, 3, 2]:
+        pieces = [(t, slice(lo, lo + N // 2)) for t in range(4) for lo in (0, N // 2)][:-1]
+        pieces = pieces + [(3, slice(N // 2, 3 * N // 4)), (3, slice(3 * N // 4, N))]
+
+        def root_of(t, c):
+            nc.scalar.activation(out=root[t][:, c], in_=ratio[t][:, c], func=ACT.Abs_reciprocal_sqrt, bias=1.0)
+
+        def square_once(t, c):
+            nc.scalar.activation(out=inv_s[t][:, c], in_=root[t][:, c], func=ACT.Square)
+
+        def square_twice(t, c):
+            nc.scalar.activation(out=inv_s2[t][:, c], in_=inv_s[t][:, c], func=ACT.Square)
+
+        def scale(t, c):
+            nc.vector.tensor_tensor(out=grad[t][:, c], in0=grad[t][:, c], in1=inv_s2[t][:, c], op=ALU.mult)
+
+        def finish(t, c):
             g, h = TILES[t]
-            for c in halves:
-                nc.scalar.activation(out=root[t][:, c], in_=ratio[t][:, c], func=ACT.Abs_reciprocal_sqrt, bias=1.0)
-            for c in halves:
-                nc.scalar.activation(out=inv_s[t][:, c], in_=root[t][:, c], func=ACT.Square)
-            if t == 3:
-                for rep in range(2):
-                    for c in halves:
-                        nc.vector.tensor_tensor(out=grad[t][:, c], in0=grad[t][:, c], in1=inv_s[t][:, c], op=ALU.mult)
-            else:
-                for c in halves:
-                    nc.scalar.activation(out=inv_s2[t][:, c], in_=inv_s[t][:, c], func=ACT.Square)
-                for c in halves:
-                    nc.vector.tensor_tensor(out=grad[t][:, c], in0=grad[t][:, c], in1=inv_s2[t][:, c], op=ALU.mult)
-            for c in halves:
-                nc.vector.tensor_tensor(out=res[t][:, c], in0=grad[t][:, c], in1=old_sb[:, col(t), c], op=ALU.add)
-            nc.sync.dma_start(out=out[g, P * h:P * (h + 1), :], in_=res[t][:])
+            nc.vector.tensor_tensor(out=res[t][:, c], in0=grad[t][:, c], in1=old_sb[:, col(t), c], op=ALU.add)
+            if t == 3 and c.stop in (N // 2, N):
+                cols = slice(c.stop - N // 2, c.stop)
+                nc.sync.dma_start(out=out[g, P * h:P * (h + 1), cols], in_=res[t][:, cols])
+            elif t < 3 and c.stop == N:
+                nc.sync.dma_start(out=out[g, P * h:P * (h + 1), :], in_=res[t][:])
+
+        stages = [root_of, square_once, square_twice, scale, finish]
+        for s in range(len(pieces) + len(stages) - 1):
+            for depth, stage in enumerate(stages):
+                if 0 <= s - depth < len(pieces):
+                    stage(*pieces[s - depth])

@@ -20,8 +20,8 @@ PACK = 4
 ROWS = D // PACK
 HALVES = M // P
 TILES = [(g, h) for h in range(HALVES) for g in range(G)]
-CHUNKS = {"x": [slice(0, N)], "dy": [slice(0, N // 2), slice(N // 2, N)]}
-X_SPLIT = 336
+CHUNKS = {"x": [slice(0, N // 2), slice(N // 2, N)], "dy": [slice(0, N // 2), slice(N // 2, N)]}
+X_SPLIT = 160
 R_CAP = 1e30
 
 
@@ -101,6 +101,7 @@ def tile_rows_btwoshare_kernel(tc, x, w1_words, w1_scales, w2_words, w2_scales, 
         nc.vector.memset(plane["wo"][:].bitcast(I32), 0)
         nc.vector.memset(re_rows[:], 0.0)
         load_act("x", 0, x)
+        load_act("x", 1, x)
         load_words(nc.sync, "w1", w1_words)
         load_plane(nc.sync, "w1", w1_scales)
         load_words(nc.sync, "w2", w2_words)
@@ -115,9 +116,10 @@ def tile_rows_btwoshare_kernel(tc, x, w1_words, w1_scales, w2_words, w2_scales, 
         load_plane(nc.sync, "wo", wo_scales)
         nc.sync.dma_start(out=old_sb[:], in_=old.rearrange("g (h p) n -> p (g h) n", p=P))
 
-        group_v("x", 0, 0, X_SPLIT)
-        group_s("x", 0, X_SPLIT, N)
-        quantize("x", 0)
+        for c in range(2):
+            group_v("x", c, 0, X_SPLIT)
+            group_s("x", c, X_SPLIT, N // 2)
+            quantize("x", c)
         group_v("dy", 0, 0, N // 2)
         quantize("dy", 0)
         group_v("dy", 1, 0, N // 2)
@@ -133,10 +135,19 @@ def tile_rows_btwoshare_kernel(tc, x, w1_words, w1_scales, w2_words, w2_scales, 
                 product(bank_a, t, "w1", "x")
             for t in pair:
                 product(bank_b, t, "w2", "x")
-            for t in pair:
-                nc.scalar.activation(out=inv_e1[t][:], in_=bank_a[t][:], func=ACT.Exp, scale=-1.0)
-            for t in pair:
-                nc.scalar.activation(out=e2[t][:], in_=bank_b[t][:], func=ACT.Exp)
+        def exp_minus_z1(t):
+            nc.scalar.activation(out=inv_e1[t][:], in_=bank_a[t][:], func=ACT.Exp, scale=-1.0)
+
+        def exp_z2(t):
+            nc.scalar.activation(out=e2[t][:], in_=bank_b[t][:], func=ACT.Exp)
+
+        exp_minus_z1(0)
+        exp_minus_z1(1)
+        exp_z2(0)
+        exp_z2(1)
+        for t in (2, 3):
+            exp_minus_z1(t)
+            exp_z2(t)
 
         def times_z3(t):
             nc.vector.scalar_tensor_tensor(out=grad[t][:], in0=ratio[t][:], scalar=R_CAP,
@@ -150,12 +161,22 @@ def tile_rows_btwoshare_kernel(tc, x, w1_words, w1_scales, w2_words, w2_scales, 
                 product(bank_a, t, "w3", "x")
             for t in pair:
                 product(bank_b, t, "wo", "dy")
-        for step, pair in [(make_ratio, (0, 1)), (times_z3, (0, 1)), (make_ratio, (2, 3)), (times_c0, (0, 1)),
-                           (times_z3, (2, 3)), (times_c0, (2, 3))]:
-            for t in pair:
-                step(t)
+        make_ratio(0)
+        make_ratio(1)
+        times_z3(0)
+        times_z3(1)
+        nc.gpsimd.tensor_scalar(out=e2[2][:], in0=e2[2][:], scalar1=re_sb[:, 32 * col(2):32 * col(2) + 1], scalar2=1.0,
+                                op0=ALU.add, op1=ALU.mult)
+        nc.gpsimd.tensor_tensor(out=ratio[2][:], in0=e2[2][:], in1=inv_e1[2][:], op=ALU.mult)
+        times_c0(0)
+        times_c0(1)
+        make_ratio(3)
+        times_z3(2)
+        times_z3(3)
+        times_c0(2)
+        times_c0(3)
 
-        pieces = [(t, slice(lo, lo + N // 2)) for t in range(4) for lo in (0, N // 2)][:-1]
+        pieces = [(t, slice(lo, lo + N // 2)) for t in range(1, 4) for lo in (0, N // 2)][:-1]
         pieces = pieces + [(3, slice(N // 2, 3 * N // 4)), (3, slice(3 * N // 4, N))]
 
         def root_of(t, c):
@@ -178,6 +199,16 @@ def tile_rows_btwoshare_kernel(tc, x, w1_words, w1_scales, w2_words, w2_scales, 
                 nc.sync.dma_start(out=out[g, P * h:P * (h + 1), cols], in_=res[t][:, cols])
             elif t < 3 and c.stop == N:
                 nc.sync.dma_start(out=out[g, P * h:P * (h + 1), :], in_=res[t][:])
+
+        halves = [slice(0, N // 2), slice(N // 2, N)]
+        for c in halves:
+            root_of(0, c)
+            nc.gpsimd.tensor_tensor(out=inv_s[0][:, c], in0=root[0][:, c], in1=root[0][:, c], op=ALU.mult)
+        for rep in range(2):
+            for c in halves:
+                nc.vector.tensor_tensor(out=grad[0][:, c], in0=grad[0][:, c], in1=inv_s[0][:, c], op=ALU.mult)
+        for c in halves:
+            finish(0, c)
 
         stages = [root_of, square_once, square_twice, scale, finish]
         for s in range(len(pieces) + len(stages) - 1):

from contextlib import ExitStack

import concourse.mybir as mybir

G, D, M, N = 2, 256, 256, 512
FLOPS = 4 * 2 * G * D * M * N

F32 = mybir.dt.float32
BF16 = mybir.dt.bfloat16
I32 = mybir.dt.int32
U32 = mybir.dt.uint32
U8 = mybir.dt.uint8
FP8X4 = mybir.dt.float8_e4m3fn_x4
FP4X4 = mybir.dt.float4_e2m1fn_x4
ACT = mybir.ActivationFunctionType
ALU = mybir.AluOpType

P = 128
PACK = 4
ROWS = D // PACK
HALVES = M // P
TILES = [(g, h) for h in range(HALVES) for g in range(G)]
CHUNKS = {"x": [slice(0, N // 2), slice(N // 2, N)], "dy": [slice(0, N // 2), slice(N // 2, N)]}
X_SPLIT = 160
R_CAP = 1e30


def tile_rows_btwoshare_kernel(tc, x, w1_words, w1_scales, w2_words, w2_scales, w3_words, w3_scales,
                                   re, wo_words, wo_scales, dy, old, out):
    nc = tc.nc
    with ExitStack() as ctx:
        sb = ctx.enter_context(tc.tile_pool(name="sb", bufs=1))
        ps = ctx.enter_context(tc.psum_pool(name="ps", bufs=1))
        ctx.enter_context(tc.manual_schedule())

        names = ["w1", "w2", "w3", "wo"]
        words = {k: sb.tile([P, 2 * M], U8, name="words_" + k, align_bytes=64) for k in names}
        acts = ["x", "dy"]
        plane = {k: sb.tile([P, N if k in acts else M], U8, name="plane_" + k, align_bytes=64) for k in names + acts}
        raw = {(k, c): sb.tile([P, PACK, cols.stop - cols.start], F32, name="raw_%s%d" % (k, c), align_bytes=64)
               for k in acts for c, cols in enumerate(CHUNKS[k])}
        grouped = {(k, c): sb.tile([P, cols.stop - cols.start, PACK], BF16, name="grouped_%s%d" % (k, c), align_bytes=64)
                   for k in acts for c, cols in enumerate(CHUNKS[k])}
        codes = {k: sb.tile([P, N], U32, name="codes_" + k, align_bytes=64) for k in acts}
        re_rows = sb.tile([P, P], F32, name="re_rows", align_bytes=64)
        re_sb = sb.tile([P, P], F32, name="re_sb", align_bytes=64)
        old_sb = sb.tile([P, G * HALVES, N], F32, name="old_sb")
        bank_a = [ps.tile([P, N], F32, name="bank_a%d" % t) for t in range(4)]
        bank_b = [ps.tile([P, N], F32, name="bank_b%d" % t) for t in range(4)]

        def work(label):
            return [sb.tile([P, N], F32, name="%s%d" % (label, t), align_bytes=64) for t in range(4)]

        inv_e1, e2, ratio, grad, root, inv_s, res = [work(s) for s in
            ["inv_e1", "e2", "ratio", "grad", "root", "inv_s", "res"]]
        inv_s2 = root

        def load_words(eng, k, src):
            eng.dma_start(out=words[k][:].bitcast(I32), in_=src.rearrange("g p b -> (g p) b").bitcast(I32))

        def load_plane(eng, k, src):
            rows = src.rearrange("g (u r) m -> r (g u) m", r=4)
            for r in range(4):
                eng.dma_start(out=plane[k][r:P:32, :].bitcast(I32), in_=rows[r].bitcast(I32))

        def load_act(k, c, src):
            nc.sync.dma_start(out=raw[k, c][:], in_=src.rearrange("g (p j) n -> (g p) j n", j=PACK)[:, :, CHUNKS[k][c]])

        def views(k, c, lo, hi):
            return (grouped[k, c][:, lo:hi, :].rearrange("p (c i) j -> p c j i", i=4),
                    raw[k, c][:, :, lo:hi].rearrange("p j (c i) -> p c j i", i=4))

        def group_v(k, c, lo, hi):
            dst, src = views(k, c, lo, hi)
            nc.vector.tensor_copy(out=dst, in_=src)

        def group_s(k, c, lo, hi):
            dst, src = views(k, c, lo, hi)
            nc.scalar.copy(out=dst, in_=src)

        def quantize(k, c):
            cols = CHUNKS[k][c]
            nc.vector.quantize_mx(out=codes[k][:, cols].bitcast(FP8X4), scales=plane[k][:, cols],
                                  in_=grouped[k, c][:].rearrange("p n j -> p (n j)"))

        def product(bank, t, w, a):
            g, h = TILES[t]
            rows = slice(ROWS * g, ROWS * (g + 1))
            nc.tensor.matmul_mx(out=bank[t][:],
                                lhsT=words[w][rows, 2 * P * h:2 * P * (h + 1)].bitcast(FP4X4),
                                lhsT_scale=plane[w][rows, P * h:P * (h + 1)],
                                rhs=codes[a][rows, :].bitcast(FP8X4), rhs_scale=plane[a][rows, :],
                                start=True, stop=True)

        def col(t):
            g, h = TILES[t]
            return HALVES * g + h

        for k in ["w1", "w2", "w3"]:
            nc.gpsimd.memset(plane[k][:].bitcast(I32), 0)
        nc.vector.memset(plane["wo"][:].bitcast(I32), 0)
        nc.vector.memset(re_rows[:], 0.0)
        load_act("x", 0, x)
        load_act("x", 1, x)
        load_words(nc.sync, "w1", w1_words)
        load_plane(nc.sync, "w1", w1_scales)
        load_words(nc.sync, "w2", w2_words)
        load_act("dy", 0, dy)
        load_plane(nc.sync, "w2", w2_scales)
        load_plane(nc.gpsimd, "w3", w3_scales)
        load_act("dy", 1, dy)
        nc.sync.dma_start(out=re_rows[0:P:32, :].rearrange("q (t i) -> q t i", i=32),
                          in_=re.rearrange("g (h q i) o -> q (g h) (i o)", q=4, i=32))
        load_words(nc.sync, "w3", w3_words)
        load_words(nc.sync, "wo", wo_words)
        load_plane(nc.sync, "wo", wo_scales)
        nc.sync.dma_start(out=old_sb[:], in_=old.rearrange("g (h p) n -> p (g h) n", p=P))

        for c in range(2):
            group_v("x", c, 0, X_SPLIT)
            group_s("x", c, X_SPLIT, N // 2)
            quantize("x", c)
        group_v("dy", 0, 0, N // 2)
        quantize("dy", 0)
        group_v("dy", 1, 0, N // 2)
        nc.vector.transpose(re_sb[:], re_rows[:])
        quantize("dy", 1)

        def make_ratio(t):
            nc.vector.scalar_tensor_tensor(out=ratio[t][:], in0=e2[t][:], scalar=re_sb[:, 32 * col(t):32 * col(t) + 1],
                                           in1=inv_e1[t][:], op0=ALU.add, op1=ALU.mult)

        for pair in [(0, 1), (2, 3)]:
            for t in pair:
                product(bank_a, t, "w1", "x")
            for t in pair:
                product(bank_b, t, "w2", "x")
        def exp_minus_z1(t):
            nc.scalar.activation(out=inv_e1[t][:], in_=bank_a[t][:], func=ACT.Exp, scale=-1.0)

        def exp_z2(t):
            nc.scalar.activation(out=e2[t][:], in_=bank_b[t][:], func=ACT.Exp)

        exp_minus_z1(0)
        exp_minus_z1(1)
        exp_z2(0)
        exp_z2(1)
        for t in (2, 3):
            exp_minus_z1(t)
            exp_z2(t)

        def times_z3(t):
            nc.vector.scalar_tensor_tensor(out=grad[t][:], in0=ratio[t][:], scalar=R_CAP,
                                           in1=bank_a[t][:], op0=ALU.min, op1=ALU.mult)

        def times_c0(t):
            nc.vector.tensor_tensor(out=grad[t][:], in0=grad[t][:], in1=bank_b[t][:], op=ALU.mult)

        for pair in [(0, 1), (2, 3)]:
            for t in pair:
                product(bank_a, t, "w3", "x")
            for t in pair:
                product(bank_b, t, "wo", "dy")
        make_ratio(0)
        make_ratio(1)
        times_z3(0)
        times_z3(1)
        nc.gpsimd.tensor_scalar(out=e2[2][:], in0=e2[2][:], scalar1=re_sb[:, 32 * col(2):32 * col(2) + 1], scalar2=1.0,
                                op0=ALU.add, op1=ALU.mult)
        nc.gpsimd.tensor_tensor(out=ratio[2][:], in0=e2[2][:], in1=inv_e1[2][:], op=ALU.mult)
        times_c0(0)
        times_c0(1)
        make_ratio(3)
        times_z3(2)
        times_z3(3)
        times_c0(2)
        times_c0(3)

        pieces = [(t, slice(lo, lo + N // 2)) for t in range(1, 4) for lo in (0, N // 2)][:-1]
        pieces = pieces + [(3, slice(N // 2, 3 * N // 4)), (3, slice(3 * N // 4, N))]

        def root_of(t, c):
            nc.scalar.activation(out=root[t][:, c], in_=ratio[t][:, c], func=ACT.Abs_reciprocal_sqrt, bias=1.0)

        def square_once(t, c):
            nc.scalar.activation(out=inv_s[t][:, c], in_=root[t][:, c], func=ACT.Square)

        def square_twice(t, c):
            nc.scalar.activation(out=inv_s2[t][:, c], in_=inv_s[t][:, c], func=ACT.Square)

        def scale(t, c):
            nc.vector.tensor_tensor(out=grad[t][:, c], in0=grad[t][:, c], in1=inv_s2[t][:, c], op=ALU.mult)

        def finish(t, c):
            g, h = TILES[t]
            nc.vector.tensor_tensor(out=res[t][:, c], in0=grad[t][:, c], in1=old_sb[:, col(t), c], op=ALU.add)
            if t == 3 and c.stop in (N // 2, N):
                cols = slice(c.stop - N // 2, c.stop)
                nc.sync.dma_start(out=out[g, P * h:P * (h + 1), cols], in_=res[t][:, cols])
            elif t < 3 and c.stop == N:
                nc.sync.dma_start(out=out[g, P * h:P * (h + 1), :], in_=res[t][:])

        halves = [slice(0, N // 2), slice(N // 2, N)]
        for c in halves:
            root_of(0, c)
            nc.gpsimd.tensor_tensor(out=inv_s[0][:, c], in0=root[0][:, c], in1=root[0][:, c], op=ALU.mult)
        for rep in range(2):
            for c in halves:
                nc.vector.tensor_tensor(out=grad[0][:, c], in0=grad[0][:, c], in1=inv_s[0][:, c], op=ALU.mult)
        for c in halves:
            finish(0, c)

        stages = [root_of, square_once, square_twice, scale, finish]
        for s in range(len(pieces) + len(stages) - 1):
            for depth, stage in enumerate(stages):
                if 0 <= s - depth < len(pieces):
                    stage(*pieces[s - depth])
